import numpy as np
import ml_dtypes


def mxq(x, axis, fmt="e4m3"):
    dtype, down = {"e4m3": (ml_dtypes.float8_e4m3fn, 7), "e5m2": (ml_dtypes.float8_e5m2, 14)}[fmt]
    v = np.moveaxis(np.asarray(x, np.float32).astype(ml_dtypes.bfloat16).astype(np.float64), axis, -1)
    blocks = v.reshape(v.shape[:-1] + (-1, 32))
    amax = np.abs(blocks).max(-1, keepdims=True)
    byte = np.maximum(np.where(amax > 0, np.frexp(amax)[1] - 1 + 127, 0) - down, 1)
    scale = np.exp2(byte - 127.0)
    codes = (blocks / scale).astype(np.float32).astype(dtype).astype(np.float64)
    return np.moveaxis((codes * scale).reshape(v.shape), -1, axis)


WIDE = False


def mx_kscale(k):
    if not WIDE:
        return np.ones(k)
    levels = np.array([10, -10, 5, -5, 0])
    if k % 512:
        return np.exp2(np.random.permutation(np.resize(levels, k // 32))).repeat(32)
    a = np.empty((k // 512, 16))
    for p in range(k // 512):
        a[p, :8] = np.random.permutation(np.resize(levels, 8))
        for g in range(8):
            far = levels[np.abs(levels - a[p, g]) >= 10]
            a[p, g + 8] = far[np.random.randint(len(far))]
    return np.exp2(a.ravel()).repeat(32)


def f64(x):
    return np.asarray(x).astype(np.float64)


def striped(idx):
    return np.tile(np.asarray(idx).reshape(-1, 16).T, (8, 1)).astype(np.uint16)


def unstriped(offs):
    return offs[:16].T.reshape(-1).astype(np.int64)


E2M1 = np.array([0.0, 0.5, 1.0, 1.5, 2.0, 3.0, 4.0, 6.0, -0.0, -0.5, -1.0, -1.5, -2.0, -3.0, -4.0, -6.0])


def pack_weight(w, fmt):
    k, n = w.shape
    w = f64(np.asarray(w, np.float32).astype(ml_dtypes.bfloat16)).reshape(k // 32, 32, n)
    amax = np.abs(w).max(1)
    if fmt == "e4m3":
        byte = np.frexp(amax)[1] - 1 + 127 - 7
    else:
        mant, ex = np.frexp(amax / 6.0)
        byte = np.where(mant > 0.5, ex, ex - 1) + 127
    byte = np.clip(np.where(amax > 0, byte, 1), 1, 254)
    scaled = (w * np.exp2(127.0 - byte)[:, None, :]).reshape(k, n).astype(np.float32)
    by_word = np.ascontiguousarray(scaled.reshape(k // 512, 128, 4, n).transpose(0, 1, 3, 2))
    if fmt == "e4m3":
        words = by_word.astype(ml_dtypes.float8_e4m3fn).view(np.uint8)
    else:
        c = by_word.astype(ml_dtypes.float4_e2m1fn).view(np.uint8) & 0xF
        words = (c[..., 0::2] | (c[..., 1::2] << 4)).reshape(k // 512, 128, 2 * n)
    return np.ascontiguousarray(words), np.ascontiguousarray(byte.astype(np.uint8).reshape(k // 512, 16, n))


def unpack_weight(words, scales, fmt):
    g, _, n = scales.shape
    words = np.ascontiguousarray(words).reshape(g, 128, n, -1)
    if fmt == "e4m3":
        vals = words.view(ml_dtypes.float8_e4m3fn).astype(np.float64)
    else:
        nib = np.empty((g, 128, n, 4), np.uint8)
        nib[..., 0::2] = words & 0xF
        nib[..., 1::2] = words >> 4
        vals = E2M1[nib]
    vals = vals * np.repeat(np.exp2(scales.astype(np.float64) - 127.0), 8, axis=1)[..., None]
    return vals.transpose(0, 1, 3, 2).reshape(g * 512, n)


def bf(x):
    return np.asarray(x, np.float32).astype(ml_dtypes.bfloat16)


def planes(Y):
    r, m = Y.shape
    b = f64(bf(Y)).reshape(r // 32, 32, m)
    amax = np.abs(b).max(1)
    byte = np.clip(np.where(amax > 0, np.frexp(amax)[1] - 1 + 127 - 7, 1), 1, 254)
    codes = (b * np.exp2(127.0 - byte)[:, None, :]).reshape(r, m).astype(np.float32).astype(ml_dtypes.float8_e4m3fn).view(np.uint8)
    words = codes.reshape(r // 512, 128, 4, m).transpose(0, 1, 3, 2)
    return np.ascontiguousarray(words), np.ascontiguousarray(byte.astype(np.uint8).reshape(r // 512, 16, m))


D, E, T, I, Q, G = 512, 512, 2048, 512, 256, 64


def setup_inputs():
    n = np.random.standard_normal
    idx = np.random.permutation(T)[:I]
    fd = mx_kscale(D)
    fi = mx_kscale(I)
    ti = np.ones(T)
    ti[idx] = fi
    keysp = pack_weight(n((D, T)) / fd[:, None], "e2m1")
    return {
        "query": (n((D, Q)) * 0.7 / np.sqrt(D) * fd[:, None]).astype(np.float32),
        "keys_words": keysp[0],
        "keys_scales": keysp[1],
        "share": (np.random.uniform(0.2, 0.8, (Q, 1))).astype(np.float32),
        "os": (np.random.uniform(4.0, 16.0, (1, I)) * fi).astype(np.float32),
        "vals": (n((E, T)) / ti).astype(np.float32),
        "offs": striped(idx),
    }


def reference(query, keys_words, keys_scales, share, os, vals, offs):
    idx = unstriped(offs)
    keysu = unpack_weight(keys_words, keys_scales, "e2m1")
    queryq = mxq(f64(query), 0, "e4m3")
    keysidxg = keysu[:, idx]
    a = queryq.T @ keysidxg
    p = np.exp(a)
    z = np.sum(p, axis=1, keepdims=True)
    s = p.reshape(Q, G, I // G).sum(axis=2)
    v1 = 1.0 / (z * f64(share) + s * (1.0 - f64(share)) * 64.0)
    vr = np.repeat(v1, I // G, axis=1)
    w = p * vr
    wo1 = w * f64(os)
    wt1 = wo1.T
    vt1 = f64(vals)[:, idx].T
    vt1q = mxq(vt1, 0, "e4m3")
    wt1q = mxq(wt1, 0, "e4m3")
    o = vt1q.T @ wt1q
    words, scales = planes(o)
    return o, words, scales

@@ -1,0 +1,230 @@
+from contextlib import ExitStack
+
+import concourse.mybir as mybir
+from concourse.masks import make_identity
+
+D, E, T, I, Q, G = 512, 512, 2048, 512, 256, 64
+FLOPS = 2 * D * Q * I + 2 * I * E * Q
+
+F32 = mybir.dt.float32
+BF16 = mybir.dt.bfloat16
+I32 = mybir.dt.int32
+U32 = mybir.dt.uint32
+U16 = mybir.dt.uint16
+U8 = mybir.dt.uint8
+FP8X4 = mybir.dt.float8_e4m3fn_x4
+FP4X4 = mybir.dt.float4_e2m1fn_x4
+ACT = mybir.ActivationFunctionType
+ALU = mybir.AluOpType
+AX = mybir.AxisListType
+
+P = 128
+PACK = 4
+GROUP = I // G
+HALVES = Q // P
+
+
+def tile_attend_mixednorm_pl_kernel(tc, query, keys_words, keys_scales, share, slot_factor, vals, offs, out_0, out_1, out_2):
+    nc = tc.nc
+    with ExitStack() as ctx:
+        sb = ctx.enter_context(tc.tile_pool(name="sb", bufs=1))
+        last = ctx.enter_context(tc.tile_pool(name="last", bufs=1))
+        ps = ctx.enter_context(tc.psum_pool(name="ps", bufs=1))
+
+        def quantize(src, width, name):
+            codes = sb.tile([P, width], U32, name=name + "_codes", align_bytes=64)
+            scales = sb.tile([P, width], U8, name=name + "_scales", align_bytes=64)
+            nc.vector.quantize_mx(out=codes[:].bitcast(FP8X4), scales=scales[:], in_=src)
+            return codes, scales
+
+        offsets = sb.tile([P, I // 16], U16, name="offsets")
+        nc.sync.dma_start(offsets[:], offs)
+
+        key_bytes = sb.tile([P, T], U8, name="key_bytes", align_bytes=64)
+        nc.vector.memset(key_bytes[:].bitcast(I32), 0)
+        for quad in range(4):
+            nc.sync.dma_start(
+                key_bytes[32 * quad : 32 * quad + 4, :].bitcast(I32),
+                keys_scales[0, 4 * quad : 4 * quad + 4, :].bitcast(I32),
+            )
+        key_words = sb.tile([P, T], U16, name="key_words", align_bytes=64)
+        nc.sync.dma_start(key_words[:].bitcast(I32), keys_words[0].bitcast(I32))
+        query_raw = sb.tile([P, PACK, Q], F32, name="query_raw")
+        nc.sync.dma_start(query_raw[:], query.rearrange("(p t) q -> p t q", t=PACK))
+
+        vals_dealt = vals.rearrange("(p t) n -> t p n", t=PACK)
+        pools = []
+        for t in range(PACK):
+            if t < PACK - 1:
+                pool_t = sb.tile([P, T], F32, name="vals_%d" % t, align_bytes=64)
+            else:
+                pool_t = last.tile([P, T], F32, name="vals_last", align_bytes=64, offset=0)
+            nc.sync.dma_start(pool_t[:], vals_dealt[t])
+            pools.append(pool_t)
+            if t == 0:
+                share_sb = sb.tile([P, HALVES, 1], F32, name="share_sb")
+                with nc.allow_non_contiguous_dma(reason="one share a partition and half"):
+                    nc.sync.dma_start(share_sb[:], share.rearrange("(h p) o -> p h o", p=P))
+                factor = sb.tile([P, 1, PACK], F32, name="factor")
+                nc.sync.dma_start(factor[:], slot_factor.rearrange("o (p t) -> p o t", t=PACK))
+
+        ident = sb.tile([P, P], F32, name="ident")
+        make_identity(nc, ident[:])
+
+        warm = sb.tile([P, 1], F32, name="warm")
+        nc.gpsimd.memset(warm[:], 0.0)
+        warm_out = sb.tile([P, 1], F32, name="warm_out")
+        nc.scalar.activation(warm_out[:], warm[:], ACT.Exp)
+
+        group_weight = sb.tile([P, HALVES, 1], F32, name="group_weight")
+        nc.vector.tensor_scalar(group_weight[:], share_sb[:], -float(G), float(G), ALU.mult, ALU.add)
+
+        listed_bytes = sb.tile([P, I], U8, name="listed_bytes", align_bytes=64)
+        nc.vector.tensor_copy(listed_bytes[:], key_bytes[:].indirect(offsets[:]))
+        listed_words = sb.tile([P, I], U16, name="listed_words", align_bytes=64)
+        nc.vector.tensor_copy(listed_words[:], key_words[:].indirect(offsets[:]))
+
+        probs = sb.tile([P, PACK, HALVES, P], F32, name="probs")
+        row_sum = []
+        probs_t = []
+        for h in range(HALVES):
+            q_bf = sb.tile([P, P, PACK], BF16, name="q_bf_%d" % h, align_bytes=64)
+            nc.scalar.copy(
+                q_bf[:].rearrange("p (c i) t -> p c t i", i=4),
+                query_raw[:, :, h * P : (h + 1) * P].rearrange("p t (c i) -> p c t i", i=4),
+            )
+            q_codes, q_scales = quantize(q_bf[:].rearrange("p q t -> p (q t)"), P, "q%d" % h)
+            scores = ps.tile([P, I], F32, name="scores_%d" % h, tag="bank_a%d" % h)
+            nc.tensor.matmul_mx(
+                out=scores[:],
+                lhsT=q_codes[:].bitcast(FP8X4),
+                lhsT_scale=q_scales[:],
+                rhs=listed_words[:].bitcast(FP4X4),
+                rhs_scale=listed_bytes[:],
+                start=True,
+                stop=True,
+            )
+            neg_max = sb.tile([P, 1], F32, name="neg_max_%d" % h)
+            nc.vector.tensor_reduce(neg_max[:], scores[:], AX.X, ALU.max, negate=True)
+            z = sb.tile([P, 1], F32, name="z_%d" % h)
+            nc.scalar.activation(
+                probs[:, :, h, :],
+                scores[:].rearrange("q (m t) -> q t m", t=PACK),
+                ACT.Exp,
+                bias=neg_max[:],
+                accum_out=z[:],
+            )
+            row_sum.append(z)
+
+        nc.scalar.activation(warm_out[:], row_sum[HALVES - 1][:], ACT.Abs_reciprocal_sqrt)
+
+        def turn_probs(h):
+            bank = ps.tile([P, PACK, P], F32, name="probs_t_%d" % h, tag="bank_p%d" % h)
+            for t in range(PACK):
+                nc.tensor.transpose(bank[:, t, :], probs[:, t, h, :], ident[:])
+            probs_t.append(bank)
+
+        turn_probs(0)
+        sums_t = ps.tile([P, P], F32, name="sums_t", tag="bank_s")
+        for t in range(PACK):
+            columns = probs[:, t, :, :].rearrange("q h m -> q (h m)")
+            for r in range(2):
+                nc.tensor.matmul(
+                    sums_t[:],
+                    lhsT=columns[:, r : 2 * P : 2],
+                    rhs=ident[:],
+                    start=(t == 0 and r == 0),
+                    stop=(t == PACK - 1 and r == 1),
+                    is_transpose=True,
+                )
+        sums_t_sb = sb.tile([P, P], F32, name="sums_t_sb")
+        nc.scalar.copy(sums_t_sb[:], sums_t[:])
+        sums = ps.tile([P, HALVES, G], F32, name="sums", tag="bank_s")
+        nc.tensor.transpose(sums[:].rearrange("q h g -> q (h g)"), sums_t_sb[:], ident[:])
+        turn_probs(1)
+
+        roots = []
+        for h in range(HALVES):
+            shared = sb.tile([P, 1], F32, name="shared_%d" % h)
+            nc.scalar.activation(shared[:], row_sum[h][:], ACT.Copy, scale=share_sb[:, h, :])
+            root = sb.tile([P, G, 1], F32, name="root_%d" % h)
+            nc.scalar.activation(
+                root[:].rearrange("q g o -> q (g o)"),
+                sums[:, h, :],
+                ACT.Abs_reciprocal_sqrt,
+                bias=shared[:],
+                scale=group_weight[:, h, :],
+            )
+            roots.append(root)
+        inverses_t = []
+        for h in range(HALVES):
+            inverse = sb.tile([P, G, 2], F32, name="inverse_%d" % h)
+            nc.scalar.activation(inverse[:], roots[h][:].to_broadcast([P, G, 2]), ACT.Square)
+            inverse_t = ps.tile([P, P], F32, name="inverse_t_%d" % h, tag="bank_a%d" % h)
+            nc.tensor.transpose(inverse_t[:], inverse[:].rearrange("q g r -> q (g r)"), ident[:])
+            inverses_t.append(inverse_t)
+
+        def listed_values(t):
+            listed = sb.tile([P, I], BF16, name="listed_%d" % t)
+            nc.vector.tensor_copy(listed[:], pools[t][:].indirect(offsets[:]))
+            words = listed[:].bitcast(F32)
+            v_t = ps.tile([P, 2, P], F32, name="v_t_%d" % t, tag="bank_v%d" % (t % 2))
+            for u in range(2):
+                nc.tensor.transpose(v_t[:, u, :], words[:, u : 2 * P : 2], ident[:])
+            v_bf = sb.tile([P, I], BF16, name="v_bf_%d" % t, align_bytes=64)
+            nc.scalar.copy(
+                v_bf[:].bitcast(F32).rearrange("m (e u) -> m e u", u=2),
+                v_t[:].rearrange("m u e -> m e u"),
+            )
+            return v_bf
+
+        turned = [listed_values(t) for t in range(PACK)]
+        w_bf = last.tile([P, Q, PACK], BF16, name="w_bf", align_bytes=64, offset=0)
+        v_codes = last.tile([P, PACK * P], U32, name="v_codes", align_bytes=64, offset=2 * Q * PACK)
+        v_scales = sb.tile([P, PACK * P], U8, name="v_scales", align_bytes=64)
+        y_codes = sb.tile([P, Q], U32, name="y_codes", align_bytes=64)
+        y_scales = sb.tile([P, Q], U8, name="y_scales", align_bytes=64)
+        out_dealt = out_0.rearrange("(p t) q -> p t q", t=PACK)
+
+        for h in range(HALVES):
+            half = slice(h * P, (h + 1) * P)
+            scaled = sb.tile([P, PACK, P], F32, name="scaled_%d" % h)
+            for t in range(PACK):
+                nc.scalar.activation(scaled[:, t, :], probs_t[h][:, t, :], ACT.Copy, scale=factor[:, 0, t : t + 1])
+            nc.vector.tensor_tensor(
+                w_bf[:, half, :].rearrange("m (c i) t -> m c t i", i=4),
+                inverses_t[h][:].rearrange("m (c o i) -> m c o i", o=1, i=4).to_broadcast([P, P // 4, PACK, 4]),
+                scaled[:].rearrange("m t (c i) -> m c t i", i=4),
+                ALU.mult,
+            )
+            w_codes, w_scales = quantize(w_bf[:, half, :].rearrange("p q t -> p (q t)"), P, "w%d" % h)
+            acc = ps.tile([P, PACK, P], F32, name="acc_%d" % h, tag="bank_p%d" % h)
+            for t in range(PACK):
+                cols = slice(t * P, (t + 1) * P)
+                if h == 0:
+                    nc.vector.quantize_mx(out=v_codes[:, cols].bitcast(FP8X4), scales=v_scales[:, cols], in_=turned[t][:])
+                nc.tensor.matmul_mx(
+                    out=acc[:, t, :],
+                    lhsT=v_codes[:, cols].bitcast(FP8X4),
+                    lhsT_scale=v_scales[:, cols],
+                    rhs=w_codes[:].bitcast(FP8X4),
+                    rhs_scale=w_scales[:],
+                    start=True,
+                    stop=True,
+                )
+            y_bf = sb.tile([P, P, PACK], BF16, name="y_bf_%d" % h, align_bytes=64)
+            nc.scalar.copy(y_bf[:], acc[:].rearrange("p t q -> p q t"))
+            nc.vector.quantize_mx(
+                out=y_codes[:, half].bitcast(FP8X4), scales=y_scales[:, half], in_=y_bf[:].rearrange("p q t -> p (q t)")
+            )
+            result = sb.tile([P, PACK, P], F32, name="result_%d" % h)
+            nc.scalar.copy(result[:], acc[:])
+            nc.sync.dma_start(out_dealt[:, :, half], result[:])
+
+        nc.sync.dma_start(out_1[0].rearrange("p c r -> p (c r)").bitcast(I32), y_codes[:].bitcast(I32))
+        for quad in range(4):
+            queue = nc.scalar if quad % 2 else nc.sync
+            queue.dma_start(
+                out_2[0, 4 * quad : 4 * quad + 4, :].bitcast(I32),
+                y_scales[32 * quad : 32 * quad + 4, :].bitcast(I32),
+            )

@@ -28,6 +28,7 @@ def tile_attend_mixednorm_pl_kernel(tc, query, keys_words, keys_scales, share, s
     nc = tc.nc
     with ExitStack() as ctx:
         sb = ctx.enter_context(tc.tile_pool(name="sb", bufs=1))
+        third = ctx.enter_context(tc.tile_pool(name="third", bufs=1))
         last = ctx.enter_context(tc.tile_pool(name="last", bufs=1))
         ps = ctx.enter_context(tc.psum_pool(name="ps", bufs=1))
 
@@ -42,11 +43,8 @@ def tile_attend_mixednorm_pl_kernel(tc, query, keys_words, keys_scales, share, s
 
         key_bytes = sb.tile([P, T], U8, name="key_bytes", align_bytes=64)
         nc.vector.memset(key_bytes[:].bitcast(I32), 0)
-        for quad in range(4):
-            nc.sync.dma_start(
-                key_bytes[32 * quad : 32 * quad + 4, :].bitcast(I32),
-                keys_scales[0, 4 * quad : 4 * quad + 4, :].bitcast(I32),
-            )
+        for row in range(4):
+            nc.sync.dma_start(key_bytes[row:P:32, :].bitcast(I32), keys_scales[0, row:16:4, :].bitcast(I32))
         key_words = sb.tile([P, T], U16, name="key_words", align_bytes=64)
         nc.sync.dma_start(key_words[:].bitcast(I32), keys_words[0].bitcast(I32))
         query_raw = sb.tile([P, PACK, Q], F32, name="query_raw")
@@ -55,16 +53,17 @@ def tile_attend_mixednorm_pl_kernel(tc, query, keys_words, keys_scales, share, s
         vals_dealt = vals.rearrange("(p t) n -> t p n", t=PACK)
         pools = []
         for t in range(PACK):
-            if t < PACK - 1:
+            if t < 2:
                 pool_t = sb.tile([P, T], F32, name="vals_%d" % t, align_bytes=64)
             else:
-                pool_t = last.tile([P, T], F32, name="vals_last", align_bytes=64, offset=0)
+                pool_t = (third, last)[t - 2].tile([P, T], F32, name="vals_%d" % t, align_bytes=64, offset=0)
             nc.sync.dma_start(pool_t[:], vals_dealt[t])
             pools.append(pool_t)
             if t == 0:
-                share_sb = sb.tile([P, HALVES, 1], F32, name="share_sb")
+                share_pad = sb.tile([P, HALVES, 8], F32, name="share_pad")
+                share_sb = share_pad[:, :, 0:1]
                 with nc.allow_non_contiguous_dma(reason="one share a partition and half"):
-                    nc.sync.dma_start(share_sb[:], share.rearrange("(h p) o -> p h o", p=P))
+                    nc.sync.dma_start(share_sb, share.rearrange("(h p) o -> p h o", p=P))
                 factor = sb.tile([P, 1, PACK], F32, name="factor")
                 nc.sync.dma_start(factor[:], slot_factor.rearrange("o (p t) -> p o t", t=PACK))
 
@@ -76,16 +75,13 @@ def tile_attend_mixednorm_pl_kernel(tc, query, keys_words, keys_scales, share, s
         warm_out = sb.tile([P, 1], F32, name="warm_out")
         nc.scalar.activation(warm_out[:], warm[:], ACT.Exp)
 
-        group_weight = sb.tile([P, HALVES, 1], F32, name="group_weight")
-        nc.vector.tensor_scalar(group_weight[:], share_sb[:], -float(G), float(G), ALU.mult, ALU.add)
-
         listed_bytes = sb.tile([P, I], U8, name="listed_bytes", align_bytes=64)
         nc.vector.tensor_copy(listed_bytes[:], key_bytes[:].indirect(offsets[:]))
         listed_words = sb.tile([P, I], U16, name="listed_words", align_bytes=64)
         nc.vector.tensor_copy(listed_words[:], key_words[:].indirect(offsets[:]))
 
         probs = sb.tile([P, PACK, HALVES, P], F32, name="probs")
-        row_sum = []
+        row_sum = sb.tile([P, HALVES, 1], F32, name="row_sum")
         probs_t = []
         for h in range(HALVES):
             q_bf = sb.tile([P, P, PACK], BF16, name="q_bf_%d" % h, align_bytes=64)
@@ -104,19 +100,17 @@ def tile_attend_mixednorm_pl_kernel(tc, query, keys_words, keys_scales, share, s
                 start=True,
                 stop=True,
             )
-            neg_max = sb.tile([P, 1], F32, name="neg_max_%d" % h)
+            neg_max = sb.tile([P, 1], F32, name="neg_max_%d" % h, tag="neg_max_%d" % h)
             nc.vector.tensor_reduce(neg_max[:], scores[:], AX.X, ALU.max, negate=True)
-            z = sb.tile([P, 1], F32, name="z_%d" % h)
             nc.scalar.activation(
                 probs[:, :, h, :],
                 scores[:].rearrange("q (m t) -> q t m", t=PACK),
                 ACT.Exp,
                 bias=neg_max[:],
-                accum_out=z[:],
+                accum_out=row_sum[:, h, :],
             )
-            row_sum.append(z)
 
-        nc.scalar.activation(warm_out[:], row_sum[HALVES - 1][:], ACT.Abs_reciprocal_sqrt)
+        nc.scalar.activation(warm_out[:], row_sum[:, HALVES - 1, :], ACT.Abs_reciprocal_sqrt)
 
         def turn_probs(h):
             bank = ps.tile([P, PACK, P], F32, name="probs_t_%d" % h, tag="bank_p%d" % h)
@@ -124,35 +118,27 @@ def tile_attend_mixednorm_pl_kernel(tc, query, keys_words, keys_scales, share, s
                 nc.tensor.transpose(bank[:, t, :], probs[:, t, h, :], ident[:])
             probs_t.append(bank)
 
-        turn_probs(0)
-        sums_t = ps.tile([P, P], F32, name="sums_t", tag="bank_s")
-        for t in range(PACK):
-            columns = probs[:, t, :, :].rearrange("q h m -> q (h m)")
-            for r in range(2):
-                nc.tensor.matmul(
-                    sums_t[:],
-                    lhsT=columns[:, r : 2 * P : 2],
-                    rhs=ident[:],
-                    start=(t == 0 and r == 0),
-                    stop=(t == PACK - 1 and r == 1),
-                    is_transpose=True,
-                )
-        sums_t_sb = sb.tile([P, P], F32, name="sums_t_sb")
-        nc.scalar.copy(sums_t_sb[:], sums_t[:])
-        sums = ps.tile([P, HALVES, G], F32, name="sums", tag="bank_s")
-        nc.tensor.transpose(sums[:].rearrange("q h g -> q (h g)"), sums_t_sb[:], ident[:])
-        turn_probs(1)
+        sums = []
+        for h in range(HALVES):
+            group_sum = sb.tile([P, G], F32, name="group_sum_%d" % h)
+            nc.vector.tensor_reduce(
+                group_sum[:], probs[:, :, h, :].rearrange("q t (g r) -> q g t r", r=2), AX.XY, ALU.add
+            )
+            sums.append(group_sum)
+            turn_probs(h)
 
+        group_weight = sb.tile([P, HALVES, 1], F32, name="group_weight", tag="neg_max_1")
+        nc.vector.tensor_scalar(group_weight[:], share_sb, -float(G), float(G), ALU.mult, ALU.add)
+        shared = sb.tile([P, HALVES, 1], F32, name="shared")
+        nc.vector.tensor_tensor(shared[:], row_sum[:], share_sb, ALU.mult)
         roots = []
         for h in range(HALVES):
-            shared = sb.tile([P, 1], F32, name="shared_%d" % h)
-            nc.scalar.activation(shared[:], row_sum[h][:], ACT.Copy, scale=share_sb[:, h, :])
             root = sb.tile([P, G, 1], F32, name="root_%d" % h)
             nc.scalar.activation(
                 root[:].rearrange("q g o -> q (g o)"),
-                sums[:, h, :],
+                sums[h][:],
                 ACT.Abs_reciprocal_sqrt,
-                bias=shared[:],
+                bias=shared[:, h, :],
                 scale=group_weight[:, h, :],
             )
             roots.append(root)
@@ -164,67 +150,99 @@ def tile_attend_mixednorm_pl_kernel(tc, query, keys_words, keys_scales, share, s
             nc.tensor.transpose(inverse_t[:], inverse[:].rearrange("q g r -> q (g r)"), ident[:])
             inverses_t.append(inverse_t)
 
-        def listed_values(t):
+        def turn_values(t, bank):
             listed = sb.tile([P, I], BF16, name="listed_%d" % t)
             nc.vector.tensor_copy(listed[:], pools[t][:].indirect(offsets[:]))
             words = listed[:].bitcast(F32)
-            v_t = ps.tile([P, 2, P], F32, name="v_t_%d" % t, tag="bank_v%d" % (t % 2))
             for u in range(2):
-                nc.tensor.transpose(v_t[:, u, :], words[:, u : 2 * P : 2], ident[:])
-            v_bf = sb.tile([P, I], BF16, name="v_bf_%d" % t, align_bytes=64)
-            nc.scalar.copy(
-                v_bf[:].bitcast(F32).rearrange("m (e u) -> m e u", u=2),
-                v_t[:].rearrange("m u e -> m e u"),
-            )
-            return v_bf
+                nc.tensor.transpose(bank[:, u, :], words[:, u : 2 * P : 2], ident[:])
 
-        turned = [listed_values(t) for t in range(PACK)]
-        w_bf = last.tile([P, Q, PACK], BF16, name="w_bf", align_bytes=64, offset=0)
-        v_codes = last.tile([P, PACK * P], U32, name="v_codes", align_bytes=64, offset=2 * Q * PACK)
-        v_scales = sb.tile([P, PACK * P], U8, name="v_scales", align_bytes=64)
-        y_codes = sb.tile([P, Q], U32, name="y_codes", align_bytes=64)
-        y_scales = sb.tile([P, Q], U8, name="y_scales", align_bytes=64)
-        out_dealt = out_0.rearrange("(p t) q -> p t q", t=PACK)
-
-        for h in range(HALVES):
-            half = slice(h * P, (h + 1) * P)
+        def weights(h, w_bf):
             scaled = sb.tile([P, PACK, P], F32, name="scaled_%d" % h)
             for t in range(PACK):
                 nc.scalar.activation(scaled[:, t, :], probs_t[h][:, t, :], ACT.Copy, scale=factor[:, 0, t : t + 1])
             nc.vector.tensor_tensor(
-                w_bf[:, half, :].rearrange("m (c i) t -> m c t i", i=4),
+                w_bf[:, h * P : (h + 1) * P, :].rearrange("m (c i) t -> m c t i", i=4),
                 inverses_t[h][:].rearrange("m (c o i) -> m c o i", o=1, i=4).to_broadcast([P, P // 4, PACK, 4]),
                 scaled[:].rearrange("m t (c i) -> m c t i", i=4),
                 ALU.mult,
             )
-            w_codes, w_scales = quantize(w_bf[:, half, :].rearrange("p q t -> p (q t)"), P, "w%d" % h)
-            acc = ps.tile([P, PACK, P], F32, name="acc_%d" % h, tag="bank_p%d" % h)
-            for t in range(PACK):
-                cols = slice(t * P, (t + 1) * P)
-                if h == 0:
-                    nc.vector.quantize_mx(out=v_codes[:, cols].bitcast(FP8X4), scales=v_scales[:, cols], in_=turned[t][:])
+
+        bank_01 = ps.tile([P, 2, 2, P], F32, name="v_t_01", tag="bank_v0")
+        bank_2 = ps.tile([P, 2, P], F32, name="v_t_2", tag="bank_v1")
+        bank_3 = ps.tile([P, 2, P], F32, name="v_t_3", tag="bank_v2")
+        turn_values(0, bank_01[:, 0])
+        turn_values(1, bank_01[:, 1])
+        turn_values(2, bank_2[:])
+        w_bf = third.tile([P, Q, PACK], BF16, name="w_bf", align_bytes=64, offset=0)
+        for h in range(HALVES):
+            weights(h, w_bf)
+        v_bf_01 = third.tile([P, 2 * I], BF16, name="v_bf_01", align_bytes=64, offset=2 * Q * PACK)
+        nc.scalar.copy(
+            v_bf_01[:].bitcast(F32).rearrange("m (t e u) -> m t e u", t=2, u=2),
+            bank_01[:].rearrange("m t u e -> m t e u"),
+        )
+        turn_values(3, bank_3[:])
+        v_bf = []
+        for t, bank in ((2, bank_2), (3, bank_3)):
+            tile = sb.tile([P, I], BF16, name="v_bf_%d" % t, align_bytes=64)
+            nc.scalar.copy(
+                tile[:].bitcast(F32).rearrange("m (e u) -> m e u", u=2), bank[:].rearrange("m u e -> m e u")
+            )
+            v_bf.append(tile)
+
+        v_codes = last.tile([P, PACK * P], U32, name="v_codes", align_bytes=64, offset=2 * I)
+        v_scales = sb.tile([P, PACK * P], U8, name="v_scales", align_bytes=64)
+
+        def quantize_values(first, count, src):
+            cols = slice(first * P, (first + count) * P)
+            nc.vector.quantize_mx(out=v_codes[:, cols].bitcast(FP8X4), scales=v_scales[:, cols], in_=src)
+
+        w_codes = last.tile([P, Q], U32, name="w_codes", align_bytes=64, offset=0)
+        w_scales = sb.tile([P, Q], U8, name="w_scales", align_bytes=64)
+        nc.vector.quantize_mx(
+            out=w_codes[:].bitcast(FP8X4), scales=w_scales[:], in_=w_bf[:].rearrange("p q t -> p (q t)")
+        )
+        quantize_values(0, 2, v_bf_01[:])
+        quantize_values(2, 1, v_bf[0][:])
+        quantize_values(3, 1, v_bf[1][:])
+
+        y_codes = sb.tile([P, Q], U32, name="y_codes", align_bytes=64)
+        y_scales = sb.tile([P, Q], U8, name="y_scales", align_bytes=64)
+        out_dealt = out_0.rearrange("(p t) q -> p t q", t=PACK)
+        accs = [ps.tile([P, PACK, P], F32, name="acc_%d" % h, tag="bank_p%d" % h) for h in range(HALVES)]
+        for t in range(PACK):
+            cols = slice(t * P, (t + 1) * P)
+            for h in range(HALVES):
+                half = slice(h * P, (h + 1) * P)
                 nc.tensor.matmul_mx(
-                    out=acc[:, t, :],
+                    out=accs[h][:, t, :],
                     lhsT=v_codes[:, cols].bitcast(FP8X4),
                     lhsT_scale=v_scales[:, cols],
-                    rhs=w_codes[:].bitcast(FP8X4),
-                    rhs_scale=w_scales[:],
+                    rhs=w_codes[:, half].bitcast(FP8X4),
+                    rhs_scale=w_scales[:, half],
                     start=True,
                     stop=True,
                 )
-            y_bf = sb.tile([P, P, PACK], BF16, name="y_bf_%d" % h, align_bytes=64)
-            nc.scalar.copy(y_bf[:], acc[:].rearrange("p t q -> p q t"))
+        y_bf = []
+        for h, round_out in enumerate((nc.scalar.copy, nc.vector.tensor_copy)):
+            tile = sb.tile([P, P, PACK], BF16, name="y_bf_%d" % h, align_bytes=64)
+            round_out(tile[:], accs[h][:].rearrange("p t q -> p q t"))
+            y_bf.append(tile)
+        for h in range(HALVES):
+            half = slice(h * P, (h + 1) * P)
             nc.vector.quantize_mx(
-                out=y_codes[:, half].bitcast(FP8X4), scales=y_scales[:, half], in_=y_bf[:].rearrange("p q t -> p (q t)")
+                out=y_codes[:, half].bitcast(FP8X4),
+                scales=y_scales[:, half],
+                in_=y_bf[h][:].rearrange("p q t -> p (q t)"),
             )
             result = sb.tile([P, PACK, P], F32, name="result_%d" % h)
-            nc.scalar.copy(result[:], acc[:])
-            nc.sync.dma_start(out_dealt[:, :, half], result[:])
+            nc.scalar.copy(result[:], accs[h][:])
+            (nc.sync, nc.scalar)[h].dma_start(out_dealt[:, :, half], result[:])
 
         nc.sync.dma_start(out_1[0].rearrange("p c r -> p (c r)").bitcast(I32), y_codes[:].bitcast(I32))
         for quad in range(4):
-            queue = nc.scalar if quad % 2 else nc.sync
-            queue.dma_start(
+            nc.sync.dma_start(
                 out_2[0, 4 * quad : 4 * quad + 4, :].bitcast(I32),
                 y_scales[32 * quad : 32 * quad + 4, :].bitcast(I32),
             )

@@ -1,3 +1,4 @@
+import math
 from contextlib import ExitStack
 
 import concourse.mybir as mybir
@@ -22,6 +23,7 @@ P = 128
 PACK = 4
 GROUP = I // G
 HALVES = Q // P
+SOFTNESS = 10.0
 
 
 def tile_attend_mixednorm_pl_kernel(tc, query, keys_words, keys_scales, share, slot_factor, vals, offs, out_0, out_1, out_2):
@@ -101,7 +103,21 @@ def tile_attend_mixednorm_pl_kernel(tc, query, keys_words, keys_scales, share, s
                 stop=True,
             )
             neg_max = sb.tile([P, 1], F32, name="neg_max_%d" % h, tag="neg_max_%d" % h)
-            nc.vector.tensor_reduce(neg_max[:], scores[:], AX.X, ALU.max, negate=True)
+            soft_sum = sb.tile([P, 1], F32, name="soft_sum_%d" % h)
+            nc.scalar.activation(
+                probs[:, :, h, :],
+                scores[:].rearrange("q (m t) -> q t m", t=PACK),
+                ACT.Exp,
+                scale=1.0 / SOFTNESS,
+                accum_out=soft_sum[:],
+            )
+            nc.scalar.activation(
+                neg_max[:],
+                soft_sum[:].bitcast(U32),
+                ACT.Copy,
+                scale=-SOFTNESS * math.log(2.0) / 2.0**23,
+                bias=SOFTNESS * (127.0 * math.log(2.0) + 0.5 * math.log(I)),
+            )
             nc.scalar.activation(
                 probs[:, :, h, :],
                 scores[:].rearrange("q (m t) -> q t m", t=PACK),
@@ -207,42 +223,31 @@ def tile_attend_mixednorm_pl_kernel(tc, query, keys_words, keys_scales, share, s
         quantize_values(2, 1, v_bf[0][:])
         quantize_values(3, 1, v_bf[1][:])
 
-        y_codes = sb.tile([P, Q], U32, name="y_codes", align_bytes=64)
-        y_scales = sb.tile([P, Q], U8, name="y_scales", align_bytes=64)
-        out_dealt = out_0.rearrange("(p t) q -> p t q", t=PACK)
-        accs = [ps.tile([P, PACK, P], F32, name="acc_%d" % h, tag="bank_p%d" % h) for h in range(HALVES)]
-        for t in range(PACK):
+        out_dealt = out_0.rearrange("(p t) q -> t p q", t=PACK)
+        result = sb.tile([P, PACK, Q], F32, name="result")
+        for t, tag in enumerate(("bank_p0", "bank_p1", "bank_s", "bank_a0")):
             cols = slice(t * P, (t + 1) * P)
-            for h in range(HALVES):
-                half = slice(h * P, (h + 1) * P)
-                nc.tensor.matmul_mx(
-                    out=accs[h][:, t, :],
-                    lhsT=v_codes[:, cols].bitcast(FP8X4),
-                    lhsT_scale=v_scales[:, cols],
-                    rhs=w_codes[:, half].bitcast(FP8X4),
-                    rhs_scale=w_scales[:, half],
-                    start=True,
-                    stop=True,
-                )
-        y_bf = []
-        for h, round_out in enumerate((nc.scalar.copy, nc.vector.tensor_copy)):
-            tile = sb.tile([P, P, PACK], BF16, name="y_bf_%d" % h, align_bytes=64)
-            round_out(tile[:], accs[h][:].rearrange("p t q -> p q t"))
-            y_bf.append(tile)
-        for h in range(HALVES):
-            half = slice(h * P, (h + 1) * P)
-            nc.vector.quantize_mx(
-                out=y_codes[:, half].bitcast(FP8X4),
-                scales=y_scales[:, half],
-                in_=y_bf[h][:].rearrange("p q t -> p (q t)"),
+            acc = ps.tile([P, Q], F32, name="acc_%d" % t, tag=tag)
+            nc.tensor.matmul_mx(
+                out=acc[:],
+                lhsT=v_codes[:, cols].bitcast(FP8X4),
+                lhsT_scale=v_scales[:, cols],
+                rhs=w_codes[:].bitcast(FP8X4),
+                rhs_scale=w_scales[:],
+                start=True,
+                stop=True,
             )
-            result = sb.tile([P, PACK, P], F32, name="result_%d" % h)
-            nc.scalar.copy(result[:], accs[h][:])
-            (nc.sync, nc.scalar)[h].dma_start(out_dealt[:, :, half], result[:])
-
+            nc.scalar.copy(result[:, t, :], acc[:])
+            nc.sync.dma_start(out_dealt[t], result[:, t, :])
+        y_bf = sb.tile([P, Q, PACK], BF16, name="y_bf", align_bytes=64)
+        nc.vector.tensor_copy(
+            y_bf[:].rearrange("p (c i) t -> p c t i", i=4), result[:].rearrange("p t (c i) -> p c t i", i=4)
+        )
+        y_codes, y_scales = quantize(y_bf[:].rearrange("p q t -> p (q t)"), Q, "y")
         nc.sync.dma_start(out_1[0].rearrange("p c r -> p (c r)").bitcast(I32), y_codes[:].bitcast(I32))
         for quad in range(4):
-            nc.sync.dma_start(
+            queue = nc.scalar if quad % 2 == 0 else nc.sync
+            queue.dma_start(
                 out_2[0, 4 * quad : 4 * quad + 4, :].bitcast(I32),
                 y_scales[32 * quad : 32 * quad + 4, :].bitcast(I32),
             )

import math
from contextlib import ExitStack

import concourse.mybir as mybir
from concourse.masks import make_identity

D, E, T, I, Q, G = 512, 512, 2048, 512, 256, 64
FLOPS = 2 * D * Q * I + 2 * I * E * Q

F32 = mybir.dt.float32
BF16 = mybir.dt.bfloat16
I32 = mybir.dt.int32
U32 = mybir.dt.uint32
U16 = mybir.dt.uint16
U8 = mybir.dt.uint8
FP8X4 = mybir.dt.float8_e4m3fn_x4
FP4X4 = mybir.dt.float4_e2m1fn_x4
ACT = mybir.ActivationFunctionType
ALU = mybir.AluOpType
AX = mybir.AxisListType

P = 128
PACK = 4
GROUP = I // G
HALVES = Q // P
SOFTNESS = 10.0


def tile_attend_mixednorm_pl_kernel(tc, query, keys_words, keys_scales, share, slot_factor, vals, offs, out_0, out_1, out_2):
    nc = tc.nc
    with ExitStack() as ctx:
        sb = ctx.enter_context(tc.tile_pool(name="sb", bufs=1))
        third = ctx.enter_context(tc.tile_pool(name="third", bufs=1))
        last = ctx.enter_context(tc.tile_pool(name="last", bufs=1))
        ps = ctx.enter_context(tc.psum_pool(name="ps", bufs=1))

        def quantize(src, width, name):
            codes = sb.tile([P, width], U32, name=name + "_codes", align_bytes=64)
            scales = sb.tile([P, width], U8, name=name + "_scales", align_bytes=64)
            nc.vector.quantize_mx(out=codes[:].bitcast(FP8X4), scales=scales[:], in_=src)
            return codes, scales

        offsets = sb.tile([P, I // 16], U16, name="offsets")
        nc.sync.dma_start(offsets[:], offs)

        key_bytes = sb.tile([P, T], U8, name="key_bytes", align_bytes=64)
        nc.vector.memset(key_bytes[:].bitcast(I32), 0)
        for row in range(4):
            nc.sync.dma_start(key_bytes[row:P:32, :].bitcast(I32), keys_scales[0, row:16:4, :].bitcast(I32))
        key_words = sb.tile([P, T], U16, name="key_words", align_bytes=64)
        nc.sync.dma_start(key_words[:].bitcast(I32), keys_words[0].bitcast(I32))
        query_raw = sb.tile([P, PACK, Q], F32, name="query_raw")
        nc.sync.dma_start(query_raw[:], query.rearrange("(p t) q -> p t q", t=PACK))

        vals_dealt = vals.rearrange("(p t) n -> t p n", t=PACK)
        pools = []
        for t in range(PACK):
            if t < 2:
                pool_t = sb.tile([P, T], F32, name="vals_%d" % t, align_bytes=64)
            else:
                pool_t = (third, last)[t - 2].tile([P, T], F32, name="vals_%d" % t, align_bytes=64, offset=0)
            nc.sync.dma_start(pool_t[:], vals_dealt[t])
            pools.append(pool_t)
            if t == 0:
                share_pad = sb.tile([P, HALVES, 8], F32, name="share_pad")
                share_sb = share_pad[:, :, 0:1]
                with nc.allow_non_contiguous_dma(reason="one share a partition and half"):
                    nc.sync.dma_start(share_sb, share.rearrange("(h p) o -> p h o", p=P))
                factor = sb.tile([P, 1, PACK], F32, name="factor")
                nc.sync.dma_start(factor[:], slot_factor.rearrange("o (p t) -> p o t", t=PACK))

        ident = sb.tile([P, P], F32, name="ident")
        make_identity(nc, ident[:])

        warm = sb.tile([P, 1], F32, name="warm")
        nc.gpsimd.memset(warm[:], 0.0)
        warm_out = sb.tile([P, 1], F32, name="warm_out")
        nc.scalar.activation(warm_out[:], warm[:], ACT.Exp)

        listed_bytes = sb.tile([P, I], U8, name="listed_bytes", align_bytes=64)
        nc.vector.tensor_copy(listed_bytes[:], key_bytes[:].indirect(offsets[:]))
        listed_words = sb.tile([P, I], U16, name="listed_words", align_bytes=64)
        nc.vector.tensor_copy(listed_words[:], key_words[:].indirect(offsets[:]))

        probs = sb.tile([P, PACK, HALVES, P], F32, name="probs")
        row_sum = sb.tile([P, HALVES, 1], F32, name="row_sum")
        probs_t = []
        for h in range(HALVES):
            q_bf = sb.tile([P, P, PACK], BF16, name="q_bf_%d" % h, align_bytes=64)
            nc.scalar.copy(
                q_bf[:].rearrange("p (c i) t -> p c t i", i=4),
                query_raw[:, :, h * P : (h + 1) * P].rearrange("p t (c i) -> p c t i", i=4),
            )
            q_codes, q_scales = quantize(q_bf[:].rearrange("p q t -> p (q t)"), P, "q%d" % h)
            scores = ps.tile([P, I], F32, name="scores_%d" % h, tag="bank_a%d" % h)
            nc.tensor.matmul_mx(
                out=scores[:],
                lhsT=q_codes[:].bitcast(FP8X4),
                lhsT_scale=q_scales[:],
                rhs=listed_words[:].bitcast(FP4X4),
                rhs_scale=listed_bytes[:],
                start=True,
                stop=True,
            )
            neg_max = sb.tile([P, 1], F32, name="neg_max_%d" % h, tag="neg_max_%d" % h)
            soft_sum = sb.tile([P, 1], F32, name="soft_sum_%d" % h)
            nc.scalar.activation(
                probs[:, :, h, :],
                scores[:].rearrange("q (m t) -> q t m", t=PACK),
                ACT.Exp,
                scale=1.0 / SOFTNESS,
                accum_out=soft_sum[:],
            )
            nc.scalar.activation(
                neg_max[:],
                soft_sum[:].bitcast(U32),
                ACT.Copy,
                scale=-SOFTNESS * math.log(2.0) / 2.0**23,
                bias=SOFTNESS * (127.0 * math.log(2.0) + 0.5 * math.log(I)),
            )
            nc.scalar.activation(
                probs[:, :, h, :],
                scores[:].rearrange("q (m t) -> q t m", t=PACK),
                ACT.Exp,
                bias=neg_max[:],
                accum_out=row_sum[:, h, :],
            )

        nc.scalar.activation(warm_out[:], row_sum[:, HALVES - 1, :], ACT.Abs_reciprocal_sqrt)

        def turn_probs(h):
            bank = ps.tile([P, PACK, P], F32, name="probs_t_%d" % h, tag="bank_p%d" % h)
            for t in range(PACK):
                nc.tensor.transpose(bank[:, t, :], probs[:, t, h, :], ident[:])
            probs_t.append(bank)

        sums = []
        for h in range(HALVES):
            group_sum = sb.tile([P, G], F32, name="group_sum_%d" % h)
            nc.vector.tensor_reduce(
                group_sum[:], probs[:, :, h, :].rearrange("q t (g r) -> q g t r", r=2), AX.XY, ALU.add
            )
            sums.append(group_sum)
            turn_probs(h)

        group_weight = sb.tile([P, HALVES, 1], F32, name="group_weight", tag="neg_max_1")
        nc.vector.tensor_scalar(group_weight[:], share_sb, -float(G), float(G), ALU.mult, ALU.add)
        shared = sb.tile([P, HALVES, 1], F32, name="shared")
        nc.vector.tensor_tensor(shared[:], row_sum[:], share_sb, ALU.mult)
        roots = []
        for h in range(HALVES):
            root = sb.tile([P, G, 1], F32, name="root_%d" % h)
            nc.scalar.activation(
                root[:].rearrange("q g o -> q (g o)"),
                sums[h][:],
                ACT.Abs_reciprocal_sqrt,
                bias=shared[:, h, :],
                scale=group_weight[:, h, :],
            )
            roots.append(root)
        inverses_t = []
        for h in range(HALVES):
            inverse = sb.tile([P, G, 2], F32, name="inverse_%d" % h)
            nc.scalar.activation(inverse[:], roots[h][:].to_broadcast([P, G, 2]), ACT.Square)
            inverse_t = ps.tile([P, P], F32, name="inverse_t_%d" % h, tag="bank_a%d" % h)
            nc.tensor.transpose(inverse_t[:], inverse[:].rearrange("q g r -> q (g r)"), ident[:])
            inverses_t.append(inverse_t)

        def turn_values(t, bank):
            listed = sb.tile([P, I], BF16, name="listed_%d" % t)
            nc.vector.tensor_copy(listed[:], pools[t][:].indirect(offsets[:]))
            words = listed[:].bitcast(F32)
            for u in range(2):
                nc.tensor.transpose(bank[:, u, :], words[:, u : 2 * P : 2], ident[:])

        def weights(h, w_bf):
            scaled = sb.tile([P, PACK, P], F32, name="scaled_%d" % h)
            for t in range(PACK):
                nc.scalar.activation(scaled[:, t, :], probs_t[h][:, t, :], ACT.Copy, scale=factor[:, 0, t : t + 1])
            nc.vector.tensor_tensor(
                w_bf[:, h * P : (h + 1) * P, :].rearrange("m (c i) t -> m c t i", i=4),
                inverses_t[h][:].rearrange("m (c o i) -> m c o i", o=1, i=4).to_broadcast([P, P // 4, PACK, 4]),
                scaled[:].rearrange("m t (c i) -> m c t i", i=4),
                ALU.mult,
            )

        bank_01 = ps.tile([P, 2, 2, P], F32, name="v_t_01", tag="bank_v0")
        bank_2 = ps.tile([P, 2, P], F32, name="v_t_2", tag="bank_v1")
        bank_3 = ps.tile([P, 2, P], F32, name="v_t_3", tag="bank_v2")
        turn_values(0, bank_01[:, 0])
        turn_values(1, bank_01[:, 1])
        turn_values(2, bank_2[:])
        w_bf = third.tile([P, Q, PACK], BF16, name="w_bf", align_bytes=64, offset=0)
        for h in range(HALVES):
            weights(h, w_bf)
        v_bf_01 = third.tile([P, 2 * I], BF16, name="v_bf_01", align_bytes=64, offset=2 * Q * PACK)
        nc.scalar.copy(
            v_bf_01[:].bitcast(F32).rearrange("m (t e u) -> m t e u", t=2, u=2),
            bank_01[:].rearrange("m t u e -> m t e u"),
        )
        turn_values(3, bank_3[:])
        v_bf = []
        for t, bank in ((2, bank_2), (3, bank_3)):
            tile = sb.tile([P, I], BF16, name="v_bf_%d" % t, align_bytes=64)
            nc.scalar.copy(
                tile[:].bitcast(F32).rearrange("m (e u) -> m e u", u=2), bank[:].rearrange("m u e -> m e u")
            )
            v_bf.append(tile)

        v_codes = last.tile([P, PACK * P], U32, name="v_codes", align_bytes=64, offset=2 * I)
        v_scales = sb.tile([P, PACK * P], U8, name="v_scales", align_bytes=64)

        def quantize_values(first, count, src):
            cols = slice(first * P, (first + count) * P)
            nc.vector.quantize_mx(out=v_codes[:, cols].bitcast(FP8X4), scales=v_scales[:, cols], in_=src)

        w_codes = last.tile([P, Q], U32, name="w_codes", align_bytes=64, offset=0)
        w_scales = sb.tile([P, Q], U8, name="w_scales", align_bytes=64)
        nc.vector.quantize_mx(
            out=w_codes[:].bitcast(FP8X4), scales=w_scales[:], in_=w_bf[:].rearrange("p q t -> p (q t)")
        )
        quantize_values(0, 2, v_bf_01[:])
        quantize_values(2, 1, v_bf[0][:])
        quantize_values(3, 1, v_bf[1][:])

        out_dealt = out_0.rearrange("(p t) q -> t p q", t=PACK)
        result = sb.tile([P, PACK, Q], F32, name="result")
        for t, tag in enumerate(("bank_p0", "bank_p1", "bank_s", "bank_a0")):
            cols = slice(t * P, (t + 1) * P)
            acc = ps.tile([P, Q], F32, name="acc_%d" % t, tag=tag)
            nc.tensor.matmul_mx(
                out=acc[:],
                lhsT=v_codes[:, cols].bitcast(FP8X4),
                lhsT_scale=v_scales[:, cols],
                rhs=w_codes[:].bitcast(FP8X4),
                rhs_scale=w_scales[:],
                start=True,
                stop=True,
            )
            nc.scalar.copy(result[:, t, :], acc[:])
            nc.sync.dma_start(out_dealt[t], result[:, t, :])
        y_bf = sb.tile([P, Q, PACK], BF16, name="y_bf", align_bytes=64)
        nc.vector.tensor_copy(
            y_bf[:].rearrange("p (c i) t -> p c t i", i=4), result[:].rearrange("p t (c i) -> p c t i", i=4)
        )
        y_codes, y_scales = quantize(y_bf[:].rearrange("p q t -> p (q t)"), Q, "y")
        nc.sync.dma_start(out_1[0].rearrange("p c r -> p (c r)").bitcast(I32), y_codes[:].bitcast(I32))
        for quad in range(4):
            queue = nc.scalar if quad % 2 == 0 else nc.sync
            queue.dma_start(
                out_2[0, 4 * quad : 4 * quad + 4, :].bitcast(I32),
                y_scales[32 * quad : 32 * quad + 4, :].bitcast(I32),
            )
